import numpy as np
import ml_dtypes


def mxq(x, axis, fmt="e4m3"):
    dtype, down = {"e4m3": (ml_dtypes.float8_e4m3fn, 7), "e5m2": (ml_dtypes.float8_e5m2, 14)}[fmt]
    v = np.moveaxis(np.asarray(x, np.float32).astype(ml_dtypes.bfloat16).astype(np.float64), axis, -1)
    blocks = v.reshape(v.shape[:-1] + (-1, 32))
    amax = np.abs(blocks).max(-1, keepdims=True)
    byte = np.maximum(np.where(amax > 0, np.frexp(amax)[1] - 1 + 127, 0) - down, 1)
    scale = np.exp2(byte - 127.0)
    codes = (blocks / scale).astype(np.float32).astype(dtype).astype(np.float64)
    return np.moveaxis((codes * scale).reshape(v.shape), -1, axis)


WIDE = False


def mx_kscale(k):
    if not WIDE:
        return np.ones(k)
    levels = np.array([10, -10, 5, -5, 0])
    if k % 512:
        return np.exp2(np.random.permutation(np.resize(levels, k // 32))).repeat(32)
    a = np.empty((k // 512, 16))
    for p in range(k // 512):
        a[p, :8] = np.random.permutation(np.resize(levels, 8))
        for g in range(8):
            far = levels[np.abs(levels - a[p, g]) >= 10]
            a[p, g + 8] = far[np.random.randint(len(far))]
    return np.exp2(a.ravel()).repeat(32)


def f64(x):
    return np.asarray(x).astype(np.float64)


def striped(idx):
    return np.tile(idx.reshape(-1, 16).T, (8, 1)).astype(np.uint16)


def unstriped(offs):
    return offs[:16].T.reshape(-1).astype(np.int64)


E2M1 = np.array([0.0, 0.5, 1.0, 1.5, 2.0, 3.0, 4.0, 6.0, -0.0, -0.5, -1.0, -1.5, -2.0, -3.0, -4.0, -6.0])


def pack_weight(w, fmt):
    k, n = w.shape
    w = f64(np.asarray(w, np.float32).astype(ml_dtypes.bfloat16)).reshape(k // 32, 32, n)
    amax = np.abs(w).max(1)
    if fmt == "e4m3":
        byte = np.frexp(amax)[1] - 1 + 127 - 7
    else:
        mant, ex = np.frexp(amax / 6.0)
        byte = np.where(mant > 0.5, ex, ex - 1) + 127
    byte = np.clip(np.where(amax > 0, byte, 1), 1, 254)
    scaled = (w * np.exp2(127.0 - byte)[:, None, :]).reshape(k, n).astype(np.float32)
    by_word = np.ascontiguousarray(scaled.reshape(k // 512, 128, 4, n).transpose(0, 1, 3, 2))
    if fmt == "e4m3":
        words = by_word.astype(ml_dtypes.float8_e4m3fn).view(np.uint8)
    else:
        c = by_word.astype(ml_dtypes.float4_e2m1fn).view(np.uint8) & 0xF
        words = (c[..., 0::2] | (c[..., 1::2] << 4)).reshape(k // 512, 128, 2 * n)
    return np.ascontiguousarray(words), np.ascontiguousarray(byte.astype(np.uint8).reshape(k // 512, 16, n))


def unpack_weight(words, scales, fmt):
    g, _, n = scales.shape
    words = np.ascontiguousarray(words).reshape(g, 128, n, -1)
    if fmt == "e4m3":
        vals = words.view(ml_dtypes.float8_e4m3fn).astype(np.float64)
    else:
        nib = np.empty((g, 128, n, 4), np.uint8)
        nib[..., 0::2] = words & 0xF
        nib[..., 1::2] = words >> 4
        vals = E2M1[nib]
    vals = vals * np.repeat(np.exp2(scales.astype(np.float64) - 127.0), 8, axis=1)[..., None]
    return vals.transpose(0, 1, 3, 2).reshape(g * 512, n)


K, T, E, C, N = 128, 768, 12, 128, 1024


def by_expert(wq, xq):
    return np.concatenate([wq[e].T @ xq[:, e * C:(e + 1) * C] for e in range(E)], axis=1)


def setup_inputs():
    n = np.random.standard_normal
    s = mx_kscale(N)[:, None]
    first = np.random.permutation(np.repeat(np.arange(E), T // E))
    second = (first + 1 + np.random.permutation(np.repeat(np.arange(E - 1), -(-T // (E - 1)))[:T])) % E
    while np.bincount(second, minlength=E).max() != T // E:
        load = np.bincount(second, minlength=E); hi, lo = int(load.argmax()), int(load.argmin())
        t = np.flatnonzero((second == hi) & (first != lo))[0]; second[t] = lo
    slot_token = np.empty(E * C, np.int64); pos = np.empty((2, T), np.int64); fill = np.zeros(E, np.int64)
    place = np.stack([np.random.permutation(C) for _ in range(E)])
    for r, deal in enumerate((first, second)):
        for t in np.random.permutation(T):
            e = deal[t]; j = e * C + place[e, fill[e]]; fill[e] += 1; slot_token[j] = t; pos[r, t] = j
    g = np.random.uniform(0.2, 0.8, T)
    w_slot = np.empty(E * C); w_slot[pos[0]] = g; w_slot[pos[1]] = 1.0 - g
    w = [pack_weight(m, "e2m1") for m in n((E + 1, N, K)) / np.sqrt(N) / s[None]]
    return {
        "dyT": (n((N, T)) * s).astype(np.float32),
        "w_words": np.stack([m[0] for m in w]),
        "w_scales": np.stack([m[1] for m in w]),
        "gate": np.tile(w_slot, (N, 1)).astype(np.float32),
        "offs": striped(slot_token),
        "pos1": striped(pos[0]),
        "pos2": striped(pos[1]),
    }


def reference(dyT, w_words, w_scales, gate, offs, pos1, pos2):
    idx = unstriped(offs)
    w = np.stack([unpack_weight(w_words[e], w_scales[e], "e2m1") for e in range(E + 1)])
    gq = mxq(f64(gate) * f64(dyT)[:, idx], 0, "e4m3")
    wq = w
    ds = wq[E].T @ mxq(f64(dyT), 0, "e4m3")
    dx = by_expert(wq, gq)
    return ds + dx[:, unstriped(pos1)] + dx[:, unstriped(pos2)]

@@ -1,0 +1,239 @@
+from contextlib import ExitStack
+
+import concourse.mybir as mybir
+from concourse.masks import make_identity
+
+K, T, E, C, N = 128, 768, 12, 128, 1024
+SLOTS = E * C
+FLOPS = 2 * N * K * (SLOTS + T)
+BYTES = 4 * N * T + (E + 1) * (N * K // 2 + N * K // 32) + 4 * SLOTS + 2 * 128 * (SLOTS + 2 * T) // 16 + 4 * K * T
+
+F32 = mybir.dt.float32
+BF16 = mybir.dt.bfloat16
+I32 = mybir.dt.int32
+U32 = mybir.dt.uint32
+U16 = mybir.dt.uint16
+U8 = mybir.dt.uint8
+FP8X4 = mybir.dt.float8_e4m3fn_x4
+FP4X4 = mybir.dt.float4_e2m1fn_x4
+COPY = mybir.ActivationFunctionType.Copy
+ADD = mybir.AluOpType.add
+MULT = mybir.AluOpType.mult
+
+P = 128
+PACK = 4
+PASSES = N // (P * PACK)
+GROUP = 4
+GROUPS = E // GROUP
+WIDTH = GROUP * C
+PER_COLUMN = 16
+
+
+def tile_moe_bds_lin_none_kernel(tc, dyT, w_words, w_scales, gate, offs, pos1, pos2, out):
+    nc = tc.nc
+    with ExitStack() as ctx:
+        keep = ctx.enter_context(tc.tile_pool(name="keep", bufs=1))
+        psum = ctx.enter_context(tc.psum_pool(name="psum", bufs=1))
+
+        offs_sb = keep.tile([P, SLOTS // PER_COLUMN], U16, name="offs_sb")
+        pos1_sb = keep.tile([P, T // PER_COLUMN], U16, name="pos1_sb")
+        pos2_sb = keep.tile([P, T // PER_COLUMN], U16, name="pos2_sb")
+        identity = keep.tile([P, P], F32, name="identity")
+        gate_rows = keep.tile([P, C], F32, name="gate_rows")
+        gate_last = keep.tile([P, 2 * C], F32, name="gate_last")
+        gate_cols = keep.tile([P, E], F32, name="gate_cols")
+        w_planes = keep.tile([P, (E + 1) * PASSES, K], U8, name="w_planes", align_bytes=64)
+        dy = [keep.tile([P, PACK, T], F32, name=f"dy{a}") for a in range(PASSES)]
+        spans = [(g * GROUP, (g + 1) * GROUP) for g in range(GROUPS)] + [(E, E + 1)]
+        w_codes = [
+            keep.tile([P, (hi - lo) * PASSES, 2 * K], U8, name=f"w_codes{lo}", align_bytes=64) for lo, hi in spans
+        ]
+
+        nc.gpsimd.memset(gate_rows[:], 0.0)
+        nc.gpsimd.memset(w_planes[:].rearrange("p q k -> p (q k)").bitcast(I32), 0)
+        make_identity(nc, identity[:])
+
+        nc.sync.dma_start(offs_sb[:], offs)
+        dy_rows = dyT.rearrange("(a p j) t -> a j p t", p=P, j=PACK)
+        for a in range(PASSES):
+            for j in range(PACK):
+                nc.sync.dma_start(dy[a][:, j, :], dy_rows[a, j])
+            if a == 0:
+                nc.sync.dma_start(gate_rows[0:E, :], gate[0].rearrange("(e c) -> e c", c=C))
+        scale_rows = w_scales.rearrange("e a (q r) k -> r q (e a) k", r=4)
+        for r in range(4):
+            nc.sync.dma_start(w_planes[r:P:32, :, :].bitcast(I32), scale_rows[r].bitcast(I32))
+        for tile, (lo, hi) in zip(w_codes, spans):
+            nc.sync.dma_start(tile[:].bitcast(I32), w_words[lo:hi].rearrange("e a p b -> p (e a) b").bitcast(I32))
+        nc.sync.dma_start(gate_last[:], gate[0:P, SLOTS - 2 * C : SLOTS])
+        nc.sync.dma_start(pos1_sb[:], pos1)
+        nc.sync.dma_start(pos2_sb[:], pos2)
+
+        turn_banks = [psum.tile([P, PACK * P], F32, name=f"turn_bank{b}") for b in range(3)]
+        back_banks = [psum.tile([P, 2, 2, C], F32, name=f"back_bank{b}") for b in range(2)]
+        sum_banks = [psum.tile([P, WIDTH], F32, name=f"sum_bank{b}") for b in range(3)]
+        nc.tensor.transpose(sum_banks[0][:, 0:C], gate_rows[:], identity[:])
+        nc.scalar.copy(gate_cols[:], sum_banks[0][:, 0:E])
+
+        def stationary(e, a):
+            g = min(e // GROUP, GROUPS)
+            q = (e - spans[g][0]) * PASSES + a
+            return w_codes[g][:, q, :].bitcast(FP4X4), w_planes[:, e * PASSES + a, :]
+
+        def product(acc, e, codes, planes, cols):
+            for a in range(PASSES):
+                w, w_plane = stationary(e, a)
+                nc.tensor.matmul_mx(
+                    out=acc,
+                    lhsT=w,
+                    lhsT_scale=w_plane,
+                    rhs=codes[a][:, cols].bitcast(FP8X4),
+                    rhs_scale=planes[a][:, cols],
+                    start=(a == 0),
+                    stop=(a == PASSES - 1),
+                )
+
+        tok_codes = [keep.tile([P, T], U32, name=f"tok_codes{a}", align_bytes=64) for a in range(PASSES)]
+        tok_planes = [keep.tile([P, T], U8, name=f"tok_planes{a}", align_bytes=64) for a in range(PASSES)]
+        token_cuts = [slice(0, 512), slice(512, T)]
+        tok_bf = [
+            [keep.tile([P, (c.stop - c.start) * PACK], BF16, name=f"tok_bf{a}{c.start}", align_bytes=64) for c in token_cuts]
+            for a in range(PASSES)
+        ]
+
+        def weave_tokens(a):
+            for cut, dst in zip(token_cuts, tok_bf[a]):
+                nc.scalar.copy(
+                    dst[:].rearrange("p (c i j) -> p c j i", i=4, j=PACK),
+                    dy[a][:, :, cut].rearrange("p j (c i) -> p c j i", i=4),
+                )
+
+        def quantise_tokens(a):
+            for cut, src in zip(token_cuts, tok_bf[a]):
+                nc.vector.quantize_mx(out=tok_codes[a][:, cut].bitcast(FP8X4), scales=tok_planes[a][:, cut], in_=src[:])
+
+        steps = [(g, a) for g in range(GROUPS) for a in range(PASSES)]
+        last = len(steps) - 1
+        woven = [keep.tile([P, 2 * WIDTH], F32, name=f"woven{n}", align_bytes=64) for n in range(last)]
+        woven_last = [keep.tile([P, WIDTH], F32, name=f"woven_last{h}", align_bytes=64) for h in range(2)]
+        low = [keep.tile([P, 2 * WIDTH], F32, name=f"low{n}") for n in range(3)]
+        high = [keep.tile([P, 2 * WIDTH], F32, name=f"high{n}") for n in range(2)]
+        gated_ring = [keep.tile([P, PACK * P], BF16, name=f"gated{n}") for n in range(3)]
+        codes = [keep.tile([P, WIDTH], U32, name=f"codes{n}", align_bytes=64) for n in range(len(steps))]
+        planes = [keep.tile([P, WIDTH], U8, name=f"planes{n}", align_bytes=64) for n in range(len(steps))]
+
+        def picked(n, j, pair):
+            width = 2 * C
+            if n == last:
+                return woven[2 + pair][:, j * width : (j + 1) * width]
+            home = high[n % 2] if j >= 2 else (low[n] if n < 3 else woven[n - 3])
+            start = (j % 2) * WIDTH
+            if pair is None:
+                return home[:, start : start + WIDTH]
+            return home[:, start + pair * width : start + (pair + 1) * width]
+
+        def gather(n, pair):
+            g, a = steps[n]
+            first = g * WIDTH + (pair or 0) * 2 * C
+            count = WIDTH if pair is None else 2 * C
+            offsets = offs_sb[:, first // PER_COLUMN : (first + count) // PER_COLUMN]
+            for j in range(PACK):
+                nc.vector.tensor_copy(picked(n, j, pair), dy[a][:, j, :].indirect(offsets))
+
+        lent_banks = {(3, 1): sum_banks[0], (3, 2): sum_banks[2], (3, 3): sum_banks[1], (last, 0): sum_banks[0]}
+        lent_scratch = {(1, 2): tok_bf[1][1], (1, 3): tok_bf[1][0]}
+
+        def gate_and_weave(n, pair):
+            g = steps[n][0]
+            back = back_banks[pair]
+            for x in range(2):
+                local = 2 * pair + x
+                e = g * GROUP + local
+                unit = n * GROUP + local
+                turned = lent_banks.get((n, local), turn_banks[unit % 3])
+                for j in range(PACK):
+                    nc.tensor.transpose(
+                        turned[:, j * P : (j + 1) * P], picked(n, j, pair)[:, x * C : (x + 1) * C], identity[:]
+                    )
+                gated = lent_scratch.get((n, local), gated_ring[unit % 3])[:, 0 : PACK * P]
+                nc.scalar.activation(
+                    gated.rearrange("c (u p v) -> c u p v", u=2, v=2),
+                    turned[:].rearrange("c (u v p) -> c u p v", u=2, v=2),
+                    COPY,
+                    scale=gate_cols[:, e : e + 1],
+                )
+                for u in range(2):
+                    nc.tensor.transpose(back[:, x, u, :], gated.bitcast(F32)[:, u * P : (u + 1) * P], identity[:])
+            words = woven_last[pair][:] if n == last else woven[n][:, pair * WIDTH : (pair + 1) * WIDTH]
+            nc.scalar.copy(words.rearrange("p (x c u) -> p x c u", x=2, u=2), back[:].rearrange("p x u c -> p x c u"))
+
+        def gate_and_weave_on_vector():
+            nc.vector.tensor_tensor(
+                woven_last[1][:].bitcast(BF16).rearrange("p (c i j) -> p c j i", i=4, j=PACK),
+                woven[3][:].rearrange("p (j c i) -> p c j i", i=4, j=PACK),
+                gate_last[:].rearrange("p (c i) -> p c i", i=4).unsqueeze(2).to_broadcast([P, 2 * C // 4, PACK, 4]),
+                MULT,
+            )
+
+        def quantise(n, pair):
+            cols = slice(0, WIDTH) if pair is None else slice(pair * 2 * C, (pair + 1) * 2 * C)
+            src = woven[n] if pair is None else woven_last[pair]
+            nc.vector.quantize_mx(
+                out=codes[n][:, cols].bitcast(FP8X4), scales=planes[n][:, cols], in_=src[:].bitcast(BF16)
+            )
+
+        dx = keep.tile([P, SLOTS], F32, name="dx")
+        ds = keep.tile([P, T], F32, name="ds")
+
+        def experts(g, locals_, bank):
+            for local in locals_:
+                cols = slice(local * C, (local + 1) * C)
+                product(bank[:, cols], g * GROUP + local, codes[2 * g : 2 * g + 2], planes[2 * g : 2 * g + 2], cols)
+            lo, hi = locals_[0] * C, (locals_[-1] + 1) * C
+            nc.scalar.copy(dx[:, g * WIDTH + lo : g * WIDTH + hi], bank[:, lo:hi])
+
+        def shared_expert():
+            product(sum_banks[1][:], E, tok_codes, tok_planes, slice(0, 512))
+            nc.scalar.copy(ds[:, 0:512], sum_banks[1][:])
+            for c0 in range(512, T, C):
+                product(sum_banks[2][:, c0 - 512 : c0 - 512 + C], E, tok_codes, tok_planes, slice(c0, c0 + C))
+            nc.scalar.copy(ds[:, 512:T], sum_banks[2][:, 0 : T - 512])
+
+        weave_tokens(0)
+        for n in range(last):
+            gather(n, None)
+            if n == 1:
+                quantise_tokens(0)
+            if n >= 2:
+                quantise(n - 2, None)
+            if n == 3:
+                quantise_tokens(1)
+            for pair in range(2):
+                gate_and_weave(n, pair)
+            if n == 1:
+                weave_tokens(1)
+            if n == 3:
+                experts(0, range(GROUP), sum_banks[0])
+                shared_expert()
+        gather(last, 0)
+        quantise(last - 2, None)
+        gather(last, 1)
+        gate_and_weave(last, 0)
+        experts(1, range(GROUP), sum_banks[0])
+        gate_and_weave_on_vector()
+        quantise(last - 1, None)
+        for pair in range(2):
+            quantise(last, pair)
+            experts(2, range(2 * pair, 2 * pair + 2), sum_banks[1 + pair])
+
+        def combine(dst, positions, other, cut):
+            offsets = positions[:, cut.start // PER_COLUMN : cut.stop // PER_COLUMN]
+            nc.vector.tensor_tensor(dst[:, cut], dx[:].indirect(offsets), other[:, cut], ADD)
+
+        partial = keep.tile([P, T], F32, name="partial")
+        total = keep.tile([P, T], F32, name="total")
+        for cut in token_cuts:
+            combine(partial, pos1_sb, ds, cut)
+        for cut in token_cuts:
+            combine(total, pos2_sb, partial, cut)
+            nc.sync.dma_start(out[:, cut], total[:, cut])

@@ -1,7 +1,6 @@
 from contextlib import ExitStack
 
 import concourse.mybir as mybir
-from concourse.masks import make_identity
 
 K, T, E, C, N = 128, 768, 12, 128, 1024
 SLOTS = E * C
@@ -16,7 +15,6 @@ U16 = mybir.dt.uint16
 U8 = mybir.dt.uint8
 FP8X4 = mybir.dt.float8_e4m3fn_x4
 FP4X4 = mybir.dt.float4_e2m1fn_x4
-COPY = mybir.ActivationFunctionType.Copy
 ADD = mybir.AluOpType.add
 MULT = mybir.AluOpType.mult
 
@@ -38,42 +36,38 @@ def tile_moe_bds_lin_none_kernel(tc, dyT, w_words, w_scales, gate, offs, pos1, p
         offs_sb = keep.tile([P, SLOTS // PER_COLUMN], U16, name="offs_sb")
         pos1_sb = keep.tile([P, T // PER_COLUMN], U16, name="pos1_sb")
         pos2_sb = keep.tile([P, T // PER_COLUMN], U16, name="pos2_sb")
-        identity = keep.tile([P, P], F32, name="identity")
-        gate_rows = keep.tile([P, C], F32, name="gate_rows")
-        gate_last = keep.tile([P, 2 * C], F32, name="gate_last")
-        gate_cols = keep.tile([P, E], F32, name="gate_cols")
+        gates = [keep.tile([P, WIDTH], F32, name=f"gates{g}") for g in range(GROUPS)]
+        window = [[keep.tile([P, T], F32, name=f"window{a}{j}") for j in range(PACK)] for a in range(PASSES)]
         w_planes = keep.tile([P, (E + 1) * PASSES, K], U8, name="w_planes", align_bytes=64)
-        dy = [keep.tile([P, PACK, T], F32, name=f"dy{a}") for a in range(PASSES)]
+        dy = [keep.tile([P, PACK * T], F32, name=f"dy{a}", align_bytes=64) for a in range(PASSES)]
         spans = [(g * GROUP, (g + 1) * GROUP) for g in range(GROUPS)] + [(E, E + 1)]
         w_codes = [
             keep.tile([P, (hi - lo) * PASSES, 2 * K], U8, name=f"w_codes{lo}", align_bytes=64) for lo, hi in spans
         ]
 
-        nc.gpsimd.memset(gate_rows[:], 0.0)
         nc.gpsimd.memset(w_planes[:].rearrange("p q k -> p (q k)").bitcast(I32), 0)
-        make_identity(nc, identity[:])
 
         nc.sync.dma_start(offs_sb[:], offs)
         dy_rows = dyT.rearrange("(a p j) t -> a j p t", p=P, j=PACK)
         for a in range(PASSES):
             for j in range(PACK):
-                nc.sync.dma_start(dy[a][:, j, :], dy_rows[a, j])
+                nc.sync.dma_start(window[a][j][:], dy_rows[a, j])
+                if a == 0 and j == 0:
+                    nc.sync.dma_start(gates[0][:], gate[0:P, 0:WIDTH])
+        nc.sync.dma_start(gates[1][:], gate[0:P, WIDTH : 2 * WIDTH])
+        for a in range(PASSES):
+            nc.sync.dma_start(dy[a][:], dyT[a * P * PACK : (a + 1) * P * PACK, :].rearrange("(p j) t -> p (j t)", j=PACK))
             if a == 0:
-                nc.sync.dma_start(gate_rows[0:E, :], gate[0].rearrange("(e c) -> e c", c=C))
+                nc.sync.dma_start(gates[2][:], gate[0:P, 2 * WIDTH : 3 * WIDTH])
         scale_rows = w_scales.rearrange("e a (q r) k -> r q (e a) k", r=4)
         for r in range(4):
             nc.sync.dma_start(w_planes[r:P:32, :, :].bitcast(I32), scale_rows[r].bitcast(I32))
         for tile, (lo, hi) in zip(w_codes, spans):
             nc.sync.dma_start(tile[:].bitcast(I32), w_words[lo:hi].rearrange("e a p b -> p (e a) b").bitcast(I32))
-        nc.sync.dma_start(gate_last[:], gate[0:P, SLOTS - 2 * C : SLOTS])
         nc.sync.dma_start(pos1_sb[:], pos1)
         nc.sync.dma_start(pos2_sb[:], pos2)
 
-        turn_banks = [psum.tile([P, PACK * P], F32, name=f"turn_bank{b}") for b in range(3)]
-        back_banks = [psum.tile([P, 2, 2, C], F32, name=f"back_bank{b}") for b in range(2)]
-        sum_banks = [psum.tile([P, WIDTH], F32, name=f"sum_bank{b}") for b in range(3)]
-        nc.tensor.transpose(sum_banks[0][:, 0:C], gate_rows[:], identity[:])
-        nc.scalar.copy(gate_cols[:], sum_banks[0][:, 0:E])
+        sum_banks = [psum.tile([P, WIDTH], F32, name=f"sum_bank{b}") for b in range(7)]
 
         def stationary(e, a):
             g = min(e // GROUP, GROUPS)
@@ -105,7 +99,7 @@ def tile_moe_bds_lin_none_kernel(tc, dyT, w_words, w_scales, gate, offs, pos1, p
             for cut, dst in zip(token_cuts, tok_bf[a]):
                 nc.scalar.copy(
                     dst[:].rearrange("p (c i j) -> p c j i", i=4, j=PACK),
-                    dy[a][:, :, cut].rearrange("p j (c i) -> p c j i", i=4),
+                    dy[a][:].rearrange("p (j t) -> p j t", j=PACK)[:, :, cut].rearrange("p j (c i) -> p c j i", i=4),
                 )
 
         def quantise_tokens(a):
@@ -114,72 +108,44 @@ def tile_moe_bds_lin_none_kernel(tc, dyT, w_words, w_scales, gate, offs, pos1, p
 
         steps = [(g, a) for g in range(GROUPS) for a in range(PASSES)]
         last = len(steps) - 1
-        woven = [keep.tile([P, 2 * WIDTH], F32, name=f"woven{n}", align_bytes=64) for n in range(last)]
-        woven_last = [keep.tile([P, WIDTH], F32, name=f"woven_last{h}", align_bytes=64) for h in range(2)]
-        low = [keep.tile([P, 2 * WIDTH], F32, name=f"low{n}") for n in range(3)]
-        high = [keep.tile([P, 2 * WIDTH], F32, name=f"high{n}") for n in range(2)]
-        gated_ring = [keep.tile([P, PACK * P], BF16, name=f"gated{n}") for n in range(3)]
+        woven = [
+            dy[n - 2][:, 0 : 2 * WIDTH]
+            if n in (2, 3)
+            else keep.tile([P, 2 * WIDTH], F32, name=f"woven{n}", align_bytes=64)[:]
+            for n in range(len(steps))
+        ]
+        whole = slice(0, WIDTH)
+        last_cuts = [slice(0, 2 * C), slice(2 * C, 3 * C), slice(3 * C, WIDTH)]
+        ring = [keep.tile([P, PACK * WIDTH], F32, name=f"ring{n}") for n in range(2)]
         codes = [keep.tile([P, WIDTH], U32, name=f"codes{n}", align_bytes=64) for n in range(len(steps))]
         planes = [keep.tile([P, WIDTH], U8, name=f"planes{n}", align_bytes=64) for n in range(len(steps))]
 
-        def picked(n, j, pair):
-            width = 2 * C
-            if n == last:
-                return woven[2 + pair][:, j * width : (j + 1) * width]
-            home = high[n % 2] if j >= 2 else (low[n] if n < 3 else woven[n - 3])
-            start = (j % 2) * WIDTH
-            if pair is None:
-                return home[:, start : start + WIDTH]
-            return home[:, start + pair * width : start + (pair + 1) * width]
+        def picked(n, cut):
+            return ring[n % 2][:, PACK * cut.start : PACK * cut.stop]
 
-        def gather(n, pair):
+        def gather(n, cut):
             g, a = steps[n]
-            first = g * WIDTH + (pair or 0) * 2 * C
-            count = WIDTH if pair is None else 2 * C
-            offsets = offs_sb[:, first // PER_COLUMN : (first + count) // PER_COLUMN]
+            count = cut.stop - cut.start
+            offsets = offs_sb[:, (g * WIDTH + cut.start) // PER_COLUMN : (g * WIDTH + cut.stop) // PER_COLUMN]
             for j in range(PACK):
-                nc.vector.tensor_copy(picked(n, j, pair), dy[a][:, j, :].indirect(offsets))
-
-        lent_banks = {(3, 1): sum_banks[0], (3, 2): sum_banks[2], (3, 3): sum_banks[1], (last, 0): sum_banks[0]}
-        lent_scratch = {(1, 2): tok_bf[1][1], (1, 3): tok_bf[1][0]}
-
-        def gate_and_weave(n, pair):
-            g = steps[n][0]
-            back = back_banks[pair]
-            for x in range(2):
-                local = 2 * pair + x
-                e = g * GROUP + local
-                unit = n * GROUP + local
-                turned = lent_banks.get((n, local), turn_banks[unit % 3])
-                for j in range(PACK):
-                    nc.tensor.transpose(
-                        turned[:, j * P : (j + 1) * P], picked(n, j, pair)[:, x * C : (x + 1) * C], identity[:]
-                    )
-                gated = lent_scratch.get((n, local), gated_ring[unit % 3])[:, 0 : PACK * P]
-                nc.scalar.activation(
-                    gated.rearrange("c (u p v) -> c u p v", u=2, v=2),
-                    turned[:].rearrange("c (u v p) -> c u p v", u=2, v=2),
-                    COPY,
-                    scale=gate_cols[:, e : e + 1],
+                nc.vector.tensor_tensor(
+                    picked(n, cut)[:, j * count : (j + 1) * count],
+                    window[a][j][:].indirect(offsets),
+                    gates[g][:, cut],
+                    MULT,
                 )
-                for u in range(2):
-                    nc.tensor.transpose(back[:, x, u, :], gated.bitcast(F32)[:, u * P : (u + 1) * P], identity[:])
-            words = woven_last[pair][:] if n == last else woven[n][:, pair * WIDTH : (pair + 1) * WIDTH]
-            nc.scalar.copy(words.rearrange("p (x c u) -> p x c u", x=2, u=2), back[:].rearrange("p x u c -> p x c u"))
 
-        def gate_and_weave_on_vector():
-            nc.vector.tensor_tensor(
-                woven_last[1][:].bitcast(BF16).rearrange("p (c i j) -> p c j i", i=4, j=PACK),
-                woven[3][:].rearrange("p (j c i) -> p c j i", i=4, j=PACK),
-                gate_last[:].rearrange("p (c i) -> p c i", i=4).unsqueeze(2).to_broadcast([P, 2 * C // 4, PACK, 4]),
-                MULT,
+        def weave(n, cut):
+            nc.scalar.copy(
+                woven[n][:, 2 * cut.start : 2 * cut.stop].bitcast(BF16).rearrange("p (c i j) -> p c j i", i=4, j=PACK),
+                picked(n, cut).rearrange("p (j c i) -> p c j i", i=4, j=PACK),
             )
 
-        def quantise(n, pair):
-            cols = slice(0, WIDTH) if pair is None else slice(pair * 2 * C, (pair + 1) * 2 * C)
-            src = woven[n] if pair is None else woven_last[pair]
+        def quantise(n, cut):
             nc.vector.quantize_mx(
-                out=codes[n][:, cols].bitcast(FP8X4), scales=planes[n][:, cols], in_=src[:].bitcast(BF16)
+                out=codes[n][:, cut].bitcast(FP8X4),
+                scales=planes[n][:, cut],
+                in_=woven[n][:, 2 * cut.start : 2 * cut.stop].bitcast(BF16),
             )
 
         dx = keep.tile([P, SLOTS], F32, name="dx")
@@ -193,38 +159,32 @@ def tile_moe_bds_lin_none_kernel(tc, dyT, w_words, w_scales, gate, offs, pos1, p
             nc.scalar.copy(dx[:, g * WIDTH + lo : g * WIDTH + hi], bank[:, lo:hi])
 
         def shared_expert():
-            product(sum_banks[1][:], E, tok_codes, tok_planes, slice(0, 512))
-            nc.scalar.copy(ds[:, 0:512], sum_banks[1][:])
+            product(sum_banks[5][:], E, tok_codes, tok_planes, slice(0, 512))
+            nc.scalar.copy(ds[:, 0:512], sum_banks[5][:])
             for c0 in range(512, T, C):
-                product(sum_banks[2][:, c0 - 512 : c0 - 512 + C], E, tok_codes, tok_planes, slice(c0, c0 + C))
-            nc.scalar.copy(ds[:, 512:T], sum_banks[2][:, 0 : T - 512])
+                product(sum_banks[6][:, c0 - 512 : c0 - 512 + C], E, tok_codes, tok_planes, slice(c0, c0 + C))
+            nc.scalar.copy(ds[:, 512:T], sum_banks[6][:, 0 : T - 512])
 
-        weave_tokens(0)
         for n in range(last):
-            gather(n, None)
-            if n == 1:
-                quantise_tokens(0)
             if n >= 2:
-                quantise(n - 2, None)
-            if n == 3:
-                quantise_tokens(1)
-            for pair in range(2):
-                gate_and_weave(n, pair)
-            if n == 1:
-                weave_tokens(1)
+                quantise(n - 2, whole)
             if n == 3:
                 experts(0, range(GROUP), sum_banks[0])
-                shared_expert()
-        gather(last, 0)
-        quantise(last - 2, None)
-        gather(last, 1)
-        gate_and_weave(last, 0)
-        experts(1, range(GROUP), sum_banks[0])
-        gate_and_weave_on_vector()
-        quantise(last - 1, None)
-        for pair in range(2):
-            quantise(last, pair)
-            experts(2, range(2 * pair, 2 * pair + 2), sum_banks[1 + pair])
+            gather(n, whole)
+            if n in (2, 3):
+                weave_tokens(n - 2)
+                quantise_tokens(n - 2)
+            weave(n, whole)
+        quantise(last - 2, whole)
+        experts(1, range(GROUP), sum_banks[1])
+        shared_expert()
+        for cut in last_cuts:
+            gather(last, cut)
+            weave(last, cut)
+        quantise(last - 1, whole)
+        for x, cut in enumerate(last_cuts):
+            quantise(last, cut)
+            experts(2, range(cut.start // C, cut.stop // C), sum_banks[2 + x])
 
         def combine(dst, positions, other, cut):
             offsets = positions[:, cut.start // PER_COLUMN : cut.stop // PER_COLUMN]

@@ -49,11 +49,12 @@ def tile_moe_bds_lin_none_kernel(tc, dyT, w_words, w_scales, gate, offs, pos1, p
 
         nc.sync.dma_start(offs_sb[:], offs)
         dy_rows = dyT.rearrange("(a p j) t -> a j p t", p=P, j=PACK)
+        nc.sync.dma_start(gates[0][:, 0:C], gate[0:P, 0:C])
         for a in range(PASSES):
             for j in range(PACK):
                 nc.sync.dma_start(window[a][j][:], dy_rows[a, j])
                 if a == 0 and j == 0:
-                    nc.sync.dma_start(gates[0][:], gate[0:P, 0:WIDTH])
+                    nc.sync.dma_start(gates[0][:, C:WIDTH], gate[0:P, C:WIDTH])
         nc.sync.dma_start(gates[1][:], gate[0:P, WIDTH : 2 * WIDTH])
         for a in range(PASSES):
             nc.sync.dma_start(dy[a][:], dyT[a * P * PACK : (a + 1) * P * PACK, :].rearrange("(p j) t -> p (j t)", j=PACK))
@@ -62,20 +63,21 @@ def tile_moe_bds_lin_none_kernel(tc, dyT, w_words, w_scales, gate, offs, pos1, p
         scale_rows = w_scales.rearrange("e a (q r) k -> r q (e a) k", r=4)
         for r in range(4):
             nc.sync.dma_start(w_planes[r:P:32, :, :].bitcast(I32), scale_rows[r].bitcast(I32))
-        for tile, (lo, hi) in zip(w_codes, spans):
-            nc.sync.dma_start(tile[:].bitcast(I32), w_words[lo:hi].rearrange("e a p b -> p (e a) b").bitcast(I32))
+        for g in (0, GROUPS, 1, 2):
+            lo, hi = spans[g]
+            nc.sync.dma_start(w_codes[g][:].bitcast(I32), w_words[lo:hi].rearrange("e a p b -> p (e a) b").bitcast(I32))
         nc.sync.dma_start(pos1_sb[:], pos1)
         nc.sync.dma_start(pos2_sb[:], pos2)
 
-        sum_banks = [psum.tile([P, WIDTH], F32, name=f"sum_bank{b}") for b in range(7)]
+        sum_banks = [psum.tile([P, WIDTH], F32, name=f"sum_bank{b}") for b in range(8)]
 
         def stationary(e, a):
             g = min(e // GROUP, GROUPS)
             q = (e - spans[g][0]) * PASSES + a
             return w_codes[g][:, q, :].bitcast(FP4X4), w_planes[:, e * PASSES + a, :]
 
-        def product(acc, e, codes, planes, cols):
-            for a in range(PASSES):
+        def product(acc, e, codes, planes, cols, passes=range(PASSES)):
+            for a in passes:
                 w, w_plane = stationary(e, a)
                 nc.tensor.matmul_mx(
                     out=acc,
@@ -121,19 +123,24 @@ def tile_moe_bds_lin_none_kernel(tc, dyT, w_words, w_scales, gate, offs, pos1, p
         planes = [keep.tile([P, WIDTH], U8, name=f"planes{n}", align_bytes=64) for n in range(len(steps))]
 
         def picked(n, cut):
+            if n == last and cut != last_cuts[0]:
+                return woven[last - 1][:, PACK * (cut.start - 2 * C) : PACK * (cut.stop - 2 * C)]
             return ring[n % 2][:, PACK * cut.start : PACK * cut.stop]
 
         def gather(n, cut):
             g, a = steps[n]
             count = cut.stop - cut.start
-            offsets = offs_sb[:, (g * WIDTH + cut.start) // PER_COLUMN : (g * WIDTH + cut.stop) // PER_COLUMN]
             for j in range(PACK):
-                nc.vector.tensor_tensor(
-                    picked(n, cut)[:, j * count : (j + 1) * count],
-                    window[a][j][:].indirect(offsets),
-                    gates[g][:, cut],
-                    MULT,
-                )
+                parts = [slice(0, C), slice(C, WIDTH)] if n == 0 and j == 0 else [cut]
+                for part in parts:
+                    offsets = offs_sb[:, (g * WIDTH + part.start) // PER_COLUMN : (g * WIDTH + part.stop) // PER_COLUMN]
+                    first = j * count - cut.start
+                    nc.vector.tensor_tensor(
+                        picked(n, cut)[:, first + part.start : first + part.stop],
+                        window[a][j][:].indirect(offsets),
+                        gates[g][:, part],
+                        MULT,
+                    )
 
         def weave(n, cut):
             nc.scalar.copy(
@@ -159,11 +166,11 @@ def tile_moe_bds_lin_none_kernel(tc, dyT, w_words, w_scales, gate, offs, pos1, p
             nc.scalar.copy(dx[:, g * WIDTH + lo : g * WIDTH + hi], bank[:, lo:hi])
 
         def shared_expert():
-            product(sum_banks[5][:], E, tok_codes, tok_planes, slice(0, 512))
-            nc.scalar.copy(ds[:, 0:512], sum_banks[5][:])
+            product(sum_banks[2][:], E, tok_codes, tok_planes, slice(0, 512))
+            nc.scalar.copy(ds[:, 0:512], sum_banks[2][:])
             for c0 in range(512, T, C):
-                product(sum_banks[6][:, c0 - 512 : c0 - 512 + C], E, tok_codes, tok_planes, slice(c0, c0 + C))
-            nc.scalar.copy(ds[:, 512:T], sum_banks[6][:, 0 : T - 512])
+                product(sum_banks[3][:, c0 - 512 : c0 - 512 + C], E, tok_codes, tok_planes, slice(c0, c0 + C))
+            nc.scalar.copy(ds[:, 512:T], sum_banks[3][:, 0 : T - 512])
 
         for n in range(last):
             if n >= 2:
@@ -178,13 +185,26 @@ def tile_moe_bds_lin_none_kernel(tc, dyT, w_words, w_scales, gate, offs, pos1, p
         quantise(last - 2, whole)
         experts(1, range(GROUP), sum_banks[1])
         shared_expert()
-        for cut in last_cuts:
+        g = GROUPS - 1
+
+        def last_group(local, a):
+            cols = slice(local * C, (local + 1) * C)
+            bank = sum_banks[4 + local]
+            product(bank[:, 0:C], g * GROUP + local, codes[2 * g : 2 * g + 2], planes[2 * g : 2 * g + 2], cols, [a])
+            if a == PASSES - 1:
+                nc.scalar.copy(dx[:, g * WIDTH + cols.start : g * WIDTH + cols.stop], bank[:, 0:C])
+
+        for x, cut in enumerate(last_cuts):
+            if x == 1:
+                quantise(last - 1, whole)
+                for local in range(GROUP):
+                    last_group(local, 0)
             gather(last, cut)
             weave(last, cut)
-        quantise(last - 1, whole)
-        for x, cut in enumerate(last_cuts):
+        for cut in last_cuts:
             quantise(last, cut)
-            experts(2, range(cut.start // C, cut.stop // C), sum_banks[2 + x])
+            for local in range(cut.start // C, cut.stop // C):
+                last_group(local, 1)
 
         def combine(dst, positions, other, cut):
             offsets = positions[:, cut.start // PER_COLUMN : cut.stop // PER_COLUMN]

@@ -47,13 +47,13 @@ def tile_moe_bds_lin_none_kernel(tc, dyT, w_words, w_scales, gate, offs, pos1, p
 
         nc.gpsimd.memset(w_planes[:].rearrange("p q k -> p (q k)").bitcast(I32), 0)
 
-        nc.sync.dma_start(offs_sb[:], offs)
         dy_rows = dyT.rearrange("(a p j) t -> a j p t", p=P, j=PACK)
-        nc.sync.dma_start(gates[0][:, 0:C], gate[0:P, 0:C])
         for a in range(PASSES):
             for j in range(PACK):
                 nc.sync.dma_start(window[a][j][:], dy_rows[a, j])
                 if a == 0 and j == 0:
+                    nc.sync.dma_start(offs_sb[:], offs)
+                    nc.sync.dma_start(gates[0][:, 0:C], gate[0:P, 0:C])
                     nc.sync.dma_start(gates[0][:, C:WIDTH], gate[0:P, C:WIDTH])
         nc.sync.dma_start(gates[1][:], gate[0:P, WIDTH : 2 * WIDTH])
         for a in range(PASSES):
@@ -89,9 +89,8 @@ def tile_moe_bds_lin_none_kernel(tc, dyT, w_words, w_scales, gate, offs, pos1, p
                     stop=(a == PASSES - 1),
                 )
 
-        tok_codes = [keep.tile([P, T], U32, name=f"tok_codes{a}", align_bytes=64) for a in range(PASSES)]
-        tok_planes = [keep.tile([P, T], U8, name=f"tok_planes{a}", align_bytes=64) for a in range(PASSES)]
         token_cuts = [slice(0, 512), slice(512, T)]
+        tok_codes, tok_planes = {}, {}
         tok_bf = [
             [keep.tile([P, (c.stop - c.start) * PACK], BF16, name=f"tok_bf{a}{c.start}", align_bytes=64) for c in token_cuts]
             for a in range(PASSES)
@@ -104,9 +103,12 @@ def tile_moe_bds_lin_none_kernel(tc, dyT, w_words, w_scales, gate, offs, pos1, p
                     dy[a][:].rearrange("p (j t) -> p j t", j=PACK)[:, :, cut].rearrange("p j (c i) -> p c j i", i=4),
                 )
 
-        def quantise_tokens(a):
-            for cut, src in zip(token_cuts, tok_bf[a]):
-                nc.vector.quantize_mx(out=tok_codes[a][:, cut].bitcast(FP8X4), scales=tok_planes[a][:, cut], in_=src[:])
+        def quantise_tokens(a, x):
+            width = token_cuts[x].stop - token_cuts[x].start
+            tag = "late" if (a, x) == (1, 1) else f"tok_codes{a}{x}"
+            tok_codes[a, x] = keep.tile([P, width], U32, name=f"tok_codes{a}{x}", tag=tag, align_bytes=64)
+            tok_planes[a, x] = keep.tile([P, width], U8, name=f"tok_planes{a}{x}", align_bytes=64)
+            nc.vector.quantize_mx(out=tok_codes[a, x][:].bitcast(FP8X4), scales=tok_planes[a, x][:], in_=tok_bf[a][x][:])
 
         steps = [(g, a) for g in range(GROUPS) for a in range(PASSES)]
         last = len(steps) - 1
@@ -118,6 +120,13 @@ def tile_moe_bds_lin_none_kernel(tc, dyT, w_words, w_scales, gate, offs, pos1, p
         ]
         whole = slice(0, WIDTH)
         last_cuts = [slice(0, 2 * C), slice(2 * C, 3 * C), slice(3 * C, WIDTH)]
+        woven_end = keep.tile([P, 2 * C], F32, name="woven_end", tag="late", align_bytes=64)
+
+        def woven_words(n, cut):
+            if n == last and cut == last_cuts[-1]:
+                return woven_end[:]
+            return woven[n][:, 2 * cut.start : 2 * cut.stop]
+
         ring = [keep.tile([P, PACK * WIDTH], F32, name=f"ring{n}") for n in range(2)]
         codes = [keep.tile([P, WIDTH], U32, name=f"codes{n}", align_bytes=64) for n in range(len(steps))]
         planes = [keep.tile([P, WIDTH], U8, name=f"planes{n}", align_bytes=64) for n in range(len(steps))]
@@ -144,7 +153,7 @@ def tile_moe_bds_lin_none_kernel(tc, dyT, w_words, w_scales, gate, offs, pos1, p
 
         def weave(n, cut):
             nc.scalar.copy(
-                woven[n][:, 2 * cut.start : 2 * cut.stop].bitcast(BF16).rearrange("p (c i j) -> p c j i", i=4, j=PACK),
+                woven_words(n, cut).bitcast(BF16).rearrange("p (c i j) -> p c j i", i=4, j=PACK),
                 picked(n, cut).rearrange("p (j c i) -> p c j i", i=4, j=PACK),
             )
 
@@ -152,7 +161,7 @@ def tile_moe_bds_lin_none_kernel(tc, dyT, w_words, w_scales, gate, offs, pos1, p
             nc.vector.quantize_mx(
                 out=codes[n][:, cut].bitcast(FP8X4),
                 scales=planes[n][:, cut],
-                in_=woven[n][:, 2 * cut.start : 2 * cut.stop].bitcast(BF16),
+                in_=woven_words(n, cut).bitcast(BF16),
             )
 
         dx = keep.tile([P, SLOTS], F32, name="dx")
@@ -165,12 +174,15 @@ def tile_moe_bds_lin_none_kernel(tc, dyT, w_words, w_scales, gate, offs, pos1, p
             lo, hi = locals_[0] * C, (locals_[-1] + 1) * C
             nc.scalar.copy(dx[:, g * WIDTH + lo : g * WIDTH + hi], bank[:, lo:hi])
 
-        def shared_expert():
-            product(sum_banks[2][:], E, tok_codes, tok_planes, slice(0, 512))
-            nc.scalar.copy(ds[:, 0:512], sum_banks[2][:])
-            for c0 in range(512, T, C):
-                product(sum_banks[3][:, c0 - 512 : c0 - 512 + C], E, tok_codes, tok_planes, slice(c0, c0 + C))
-            nc.scalar.copy(ds[:, 512:T], sum_banks[3][:, 0 : T - 512])
+        def shared_expert(x):
+            cut = token_cuts[x]
+            width = cut.stop - cut.start
+            run = 512 if width == 512 else C
+            bank = sum_banks[2 + x]
+            for c0 in range(0, width, run):
+                cols = slice(c0, c0 + run)
+                product(bank[:, cols], E, [tok_codes[a, x] for a in range(PASSES)], [tok_planes[a, x] for a in range(PASSES)], cols)
+            nc.scalar.copy(ds[:, cut], bank[:, 0:width])
 
         for n in range(last):
             if n >= 2:
@@ -180,11 +192,13 @@ def tile_moe_bds_lin_none_kernel(tc, dyT, w_words, w_scales, gate, offs, pos1, p
             gather(n, whole)
             if n in (2, 3):
                 weave_tokens(n - 2)
-                quantise_tokens(n - 2)
+                quantise_tokens(n - 2, 0)
+            if n == 2:
+                quantise_tokens(0, 1)
             weave(n, whole)
         quantise(last - 2, whole)
         experts(1, range(GROUP), sum_banks[1])
-        shared_expert()
+        shared_expert(0)
         g = GROUPS - 1
 
         def last_group(local, a):
@@ -205,6 +219,8 @@ def tile_moe_bds_lin_none_kernel(tc, dyT, w_words, w_scales, gate, offs, pos1, p
             quantise(last, cut)
             for local in range(cut.start // C, cut.stop // C):
                 last_group(local, 1)
+        quantise_tokens(1, 1)
+        shared_expert(1)
 
         def combine(dst, positions, other, cut):
             offsets = positions[:, cut.start // PER_COLUMN : cut.stop // PER_COLUMN]

from contextlib import ExitStack

import concourse.mybir as mybir

K, T, E, C, N = 128, 768, 12, 128, 1024
SLOTS = E * C
FLOPS = 2 * N * K * (SLOTS + T)
BYTES = 4 * N * T + (E + 1) * (N * K // 2 + N * K // 32) + 4 * SLOTS + 2 * 128 * (SLOTS + 2 * T) // 16 + 4 * K * T

F32 = mybir.dt.float32
BF16 = mybir.dt.bfloat16
I32 = mybir.dt.int32
U32 = mybir.dt.uint32
U16 = mybir.dt.uint16
U8 = mybir.dt.uint8
FP8X4 = mybir.dt.float8_e4m3fn_x4
FP4X4 = mybir.dt.float4_e2m1fn_x4
ADD = mybir.AluOpType.add
MULT = mybir.AluOpType.mult

P = 128
PACK = 4
PASSES = N // (P * PACK)
GROUP = 4
GROUPS = E // GROUP
WIDTH = GROUP * C
PER_COLUMN = 16


def tile_moe_bds_lin_none_kernel(tc, dyT, w_words, w_scales, gate, offs, pos1, pos2, out):
    nc = tc.nc
    with ExitStack() as ctx:
        keep = ctx.enter_context(tc.tile_pool(name="keep", bufs=1))
        psum = ctx.enter_context(tc.psum_pool(name="psum", bufs=1))

        offs_sb = keep.tile([P, SLOTS // PER_COLUMN], U16, name="offs_sb")
        pos1_sb = keep.tile([P, T // PER_COLUMN], U16, name="pos1_sb")
        pos2_sb = keep.tile([P, T // PER_COLUMN], U16, name="pos2_sb")
        gates = [keep.tile([P, WIDTH], F32, name=f"gates{g}") for g in range(GROUPS)]
        window = [[keep.tile([P, T], F32, name=f"window{a}{j}") for j in range(PACK)] for a in range(PASSES)]
        w_planes = keep.tile([P, (E + 1) * PASSES, K], U8, name="w_planes", align_bytes=64)
        dy = [keep.tile([P, PACK * T], F32, name=f"dy{a}", align_bytes=64) for a in range(PASSES)]
        spans = [(g * GROUP, (g + 1) * GROUP) for g in range(GROUPS)] + [(E, E + 1)]
        w_codes = [
            keep.tile([P, (hi - lo) * PASSES, 2 * K], U8, name=f"w_codes{lo}", align_bytes=64) for lo, hi in spans
        ]

        nc.gpsimd.memset(w_planes[:].rearrange("p q k -> p (q k)").bitcast(I32), 0)

        dy_rows = dyT.rearrange("(a p j) t -> a j p t", p=P, j=PACK)
        for a in range(PASSES):
            for j in range(PACK):
                nc.sync.dma_start(window[a][j][:], dy_rows[a, j])
                if a == 0 and j == 0:
                    nc.sync.dma_start(offs_sb[:], offs)
                    nc.sync.dma_start(gates[0][:, 0:C], gate[0:P, 0:C])
                    nc.sync.dma_start(gates[0][:, C:WIDTH], gate[0:P, C:WIDTH])
        nc.sync.dma_start(gates[1][:], gate[0:P, WIDTH : 2 * WIDTH])
        for a in range(PASSES):
            nc.sync.dma_start(dy[a][:], dyT[a * P * PACK : (a + 1) * P * PACK, :].rearrange("(p j) t -> p (j t)", j=PACK))
            if a == 0:
                nc.sync.dma_start(gates[2][:], gate[0:P, 2 * WIDTH : 3 * WIDTH])
        scale_rows = w_scales.rearrange("e a (q r) k -> r q (e a) k", r=4)
        for r in range(4):
            nc.sync.dma_start(w_planes[r:P:32, :, :].bitcast(I32), scale_rows[r].bitcast(I32))
        for g in (0, GROUPS, 1, 2):
            lo, hi = spans[g]
            nc.sync.dma_start(w_codes[g][:].bitcast(I32), w_words[lo:hi].rearrange("e a p b -> p (e a) b").bitcast(I32))
        nc.sync.dma_start(pos1_sb[:], pos1)
        nc.sync.dma_start(pos2_sb[:], pos2)

        sum_banks = [psum.tile([P, WIDTH], F32, name=f"sum_bank{b}") for b in range(8)]

        def stationary(e, a):
            g = min(e // GROUP, GROUPS)
            q = (e - spans[g][0]) * PASSES + a
            return w_codes[g][:, q, :].bitcast(FP4X4), w_planes[:, e * PASSES + a, :]

        def product(acc, e, codes, planes, cols, passes=range(PASSES)):
            for a in passes:
                w, w_plane = stationary(e, a)
                nc.tensor.matmul_mx(
                    out=acc,
                    lhsT=w,
                    lhsT_scale=w_plane,
                    rhs=codes[a][:, cols].bitcast(FP8X4),
                    rhs_scale=planes[a][:, cols],
                    start=(a == 0),
                    stop=(a == PASSES - 1),
                )

        token_cuts = [slice(0, 512), slice(512, T)]
        tok_codes, tok_planes = {}, {}
        tok_bf = [
            [keep.tile([P, (c.stop - c.start) * PACK], BF16, name=f"tok_bf{a}{c.start}", align_bytes=64) for c in token_cuts]
            for a in range(PASSES)
        ]

        def weave_tokens(a):
            for cut, dst in zip(token_cuts, tok_bf[a]):
                nc.scalar.copy(
                    dst[:].rearrange("p (c i j) -> p c j i", i=4, j=PACK),
                    dy[a][:].rearrange("p (j t) -> p j t", j=PACK)[:, :, cut].rearrange("p j (c i) -> p c j i", i=4),
                )

        def quantise_tokens(a, x):
            width = token_cuts[x].stop - token_cuts[x].start
            tag = "late" if (a, x) == (1, 1) else f"tok_codes{a}{x}"
            tok_codes[a, x] = keep.tile([P, width], U32, name=f"tok_codes{a}{x}", tag=tag, align_bytes=64)
            tok_planes[a, x] = keep.tile([P, width], U8, name=f"tok_planes{a}{x}", align_bytes=64)
            nc.vector.quantize_mx(out=tok_codes[a, x][:].bitcast(FP8X4), scales=tok_planes[a, x][:], in_=tok_bf[a][x][:])

        steps = [(g, a) for g in range(GROUPS) for a in range(PASSES)]
        last = len(steps) - 1
        woven = [
            dy[n - 2][:, 0 : 2 * WIDTH]
            if n in (2, 3)
            else keep.tile([P, 2 * WIDTH], F32, name=f"woven{n}", align_bytes=64)[:]
            for n in range(len(steps))
        ]
        whole = slice(0, WIDTH)
        last_cuts = [slice(0, 2 * C), slice(2 * C, 3 * C), slice(3 * C, WIDTH)]
        woven_end = keep.tile([P, 2 * C], F32, name="woven_end", tag="late", align_bytes=64)

        def woven_words(n, cut):
            if n == last and cut == last_cuts[-1]:
                return woven_end[:]
            return woven[n][:, 2 * cut.start : 2 * cut.stop]

        ring = [keep.tile([P, PACK * WIDTH], F32, name=f"ring{n}") for n in range(2)]
        codes = [keep.tile([P, WIDTH], U32, name=f"codes{n}", align_bytes=64) for n in range(len(steps))]
        planes = [keep.tile([P, WIDTH], U8, name=f"planes{n}", align_bytes=64) for n in range(len(steps))]

        def picked(n, cut):
            if n == last and cut != last_cuts[0]:
                return woven[last - 1][:, PACK * (cut.start - 2 * C) : PACK * (cut.stop - 2 * C)]
            return ring[n % 2][:, PACK * cut.start : PACK * cut.stop]

        def gather(n, cut):
            g, a = steps[n]
            count = cut.stop - cut.start
            for j in range(PACK):
                parts = [slice(0, C), slice(C, WIDTH)] if n == 0 and j == 0 else [cut]
                for part in parts:
                    offsets = offs_sb[:, (g * WIDTH + part.start) // PER_COLUMN : (g * WIDTH + part.stop) // PER_COLUMN]
                    first = j * count - cut.start
                    nc.vector.tensor_tensor(
                        picked(n, cut)[:, first + part.start : first + part.stop],
                        window[a][j][:].indirect(offsets),
                        gates[g][:, part],
                        MULT,
                    )

        def weave(n, cut):
            nc.scalar.copy(
                woven_words(n, cut).bitcast(BF16).rearrange("p (c i j) -> p c j i", i=4, j=PACK),
                picked(n, cut).rearrange("p (j c i) -> p c j i", i=4, j=PACK),
            )

        def quantise(n, cut):
            nc.vector.quantize_mx(
                out=codes[n][:, cut].bitcast(FP8X4),
                scales=planes[n][:, cut],
                in_=woven_words(n, cut).bitcast(BF16),
            )

        dx = keep.tile([P, SLOTS], F32, name="dx")
        ds = keep.tile([P, T], F32, name="ds")

        def experts(g, locals_, bank):
            for local in locals_:
                cols = slice(local * C, (local + 1) * C)
                product(bank[:, cols], g * GROUP + local, codes[2 * g : 2 * g + 2], planes[2 * g : 2 * g + 2], cols)
            lo, hi = locals_[0] * C, (locals_[-1] + 1) * C
            nc.scalar.copy(dx[:, g * WIDTH + lo : g * WIDTH + hi], bank[:, lo:hi])

        def shared_expert(x):
            cut = token_cuts[x]
            width = cut.stop - cut.start
            run = 512 if width == 512 else C
            bank = sum_banks[2 + x]
            for c0 in range(0, width, run):
                cols = slice(c0, c0 + run)
                product(bank[:, cols], E, [tok_codes[a, x] for a in range(PASSES)], [tok_planes[a, x] for a in range(PASSES)], cols)
            nc.scalar.copy(ds[:, cut], bank[:, 0:width])

        for n in range(last):
            if n >= 2:
                quantise(n - 2, whole)
            if n == 3:
                experts(0, range(GROUP), sum_banks[0])
            gather(n, whole)
            if n in (2, 3):
                weave_tokens(n - 2)
                quantise_tokens(n - 2, 0)
            if n == 2:
                quantise_tokens(0, 1)
            weave(n, whole)
        quantise(last - 2, whole)
        experts(1, range(GROUP), sum_banks[1])
        shared_expert(0)
        g = GROUPS - 1

        def last_group(local, a):
            cols = slice(local * C, (local + 1) * C)
            bank = sum_banks[4 + local]
            product(bank[:, 0:C], g * GROUP + local, codes[2 * g : 2 * g + 2], planes[2 * g : 2 * g + 2], cols, [a])
            if a == PASSES - 1:
                nc.scalar.copy(dx[:, g * WIDTH + cols.start : g * WIDTH + cols.stop], bank[:, 0:C])

        for x, cut in enumerate(last_cuts):
            if x == 1:
                quantise(last - 1, whole)
                for local in range(GROUP):
                    last_group(local, 0)
            gather(last, cut)
            weave(last, cut)
        for cut in last_cuts:
            quantise(last, cut)
            for local in range(cut.start // C, cut.stop // C):
                last_group(local, 1)
        quantise_tokens(1, 1)
        shared_expert(1)

        def combine(dst, positions, other, cut):
            offsets = positions[:, cut.start // PER_COLUMN : cut.stop // PER_COLUMN]
            nc.vector.tensor_tensor(dst[:, cut], dx[:].indirect(offsets), other[:, cut], ADD)

        partial = keep.tile([P, T], F32, name="partial")
        total = keep.tile([P, T], F32, name="total")
        for cut in token_cuts:
            combine(partial, pos1_sb, ds, cut)
        for cut in token_cuts:
            combine(total, pos2_sb, partial, cut)
            nc.sync.dma_start(out[:, cut], total[:, cut])
